import numpy as np
import ml_dtypes


def mxq(x, axis, fmt="e4m3"):
    dtype, down = {"e4m3": (ml_dtypes.float8_e4m3fn, 7), "e5m2": (ml_dtypes.float8_e5m2, 14)}[fmt]
    v = np.moveaxis(np.asarray(x, np.float32).astype(ml_dtypes.bfloat16).astype(np.float64), axis, -1)
    blocks = v.reshape(v.shape[:-1] + (-1, 32))
    amax = np.abs(blocks).max(-1, keepdims=True)
    byte = np.maximum(np.where(amax > 0, np.frexp(amax)[1] - 1 + 127, 0) - down, 1)
    scale = np.exp2(byte - 127.0)
    codes = (blocks / scale).astype(np.float32).astype(dtype).astype(np.float64)
    return np.moveaxis((codes * scale).reshape(v.shape), -1, axis)


WIDE = False


def mx_kscale(k):
    if not WIDE:
        return np.ones(k)
    levels = np.array([10, -10, 5, -5, 0])
    if k % 512:
        return np.exp2(np.random.permutation(np.resize(levels, k // 32))).repeat(32)
    a = np.empty((k // 512, 16))
    for p in range(k // 512):
        a[p, :8] = np.random.permutation(np.resize(levels, 8))
        for g in range(8):
            far = levels[np.abs(levels - a[p, g]) >= 10]
            a[p, g + 8] = far[np.random.randint(len(far))]
    return np.exp2(a.ravel()).repeat(32)


def f64(x):
    return np.asarray(x).astype(np.float64)


def striped(idx):
    return np.tile(np.asarray(idx).reshape(-1, 16).T, (8, 1)).astype(np.uint16)


def unstriped(offs):
    return offs[:16].T.reshape(-1).astype(np.int64)


E2M1 = np.array([0.0, 0.5, 1.0, 1.5, 2.0, 3.0, 4.0, 6.0, -0.0, -0.5, -1.0, -1.5, -2.0, -3.0, -4.0, -6.0])


def pack_weight(w, fmt):
    k, n = w.shape
    w = f64(np.asarray(w, np.float32).astype(ml_dtypes.bfloat16)).reshape(k // 32, 32, n)
    amax = np.abs(w).max(1)
    if fmt == "e4m3":
        byte = np.frexp(amax)[1] - 1 + 127 - 7
    else:
        mant, ex = np.frexp(amax / 6.0)
        byte = np.where(mant > 0.5, ex, ex - 1) + 127
    byte = np.clip(np.where(amax > 0, byte, 1), 1, 254)
    scaled = (w * np.exp2(127.0 - byte)[:, None, :]).reshape(k, n).astype(np.float32)
    by_word = np.ascontiguousarray(scaled.reshape(k // 512, 128, 4, n).transpose(0, 1, 3, 2))
    if fmt == "e4m3":
        words = by_word.astype(ml_dtypes.float8_e4m3fn).view(np.uint8)
    else:
        c = by_word.astype(ml_dtypes.float4_e2m1fn).view(np.uint8) & 0xF
        words = (c[..., 0::2] | (c[..., 1::2] << 4)).reshape(k // 512, 128, 2 * n)
    return np.ascontiguousarray(words), np.ascontiguousarray(byte.astype(np.uint8).reshape(k // 512, 16, n))


def unpack_weight(words, scales, fmt):
    g, _, n = scales.shape
    words = np.ascontiguousarray(words).reshape(g, 128, n, -1)
    if fmt == "e4m3":
        vals = words.view(ml_dtypes.float8_e4m3fn).astype(np.float64)
    else:
        nib = np.empty((g, 128, n, 4), np.uint8)
        nib[..., 0::2] = words & 0xF
        nib[..., 1::2] = words >> 4
        vals = E2M1[nib]
    vals = vals * np.repeat(np.exp2(scales.astype(np.float64) - 127.0), 8, axis=1)[..., None]
    return vals.transpose(0, 1, 3, 2).reshape(g * 512, n)


def softplus(v):
    return np.log(1.0 + np.exp(v))


def sigmoid(v):
    return 1.0 / (1.0 + np.exp(-v))


D, E, T, I, Q = 512, 512, 2048, 512, 128


def setup_inputs():
    n = np.random.standard_normal
    idx = np.random.permutation(T)[:I]
    fd = mx_kscale(D)
    fe = mx_kscale(E)
    keysp = pack_weight(n((D, T)) / fd[:, None], "e4m3")
    valsp = pack_weight(n((E, T)) / fe[:, None], "e4m3")
    return {
        "query": (n((D, Q)) * 1.0 / np.sqrt(D) * fd[:, None]).astype(np.float32),
        "keys_words": keysp[0],
        "keys_scales": keysp[1],
        "th": (np.random.uniform(-0.5, 0.5, (Q, 1))).astype(np.float32),
        "reserve": (np.random.uniform(20.0, 100.0, (Q, 1))).astype(np.float32),
        "gout": (n((E, Q)) * 1 / np.sqrt(E) * fe[:, None]).astype(np.float32),
        "vals_words": valsp[0],
        "vals_scales": valsp[1],
        "size": (np.random.uniform(0.5, 2.0, (1, I))).astype(np.float32),
        "base": (0.5 * n((Q, I))).astype(np.float32),
        "offs": striped(idx),
    }


def reference(query, keys_words, keys_scales, th, reserve, gout, vals_words, vals_scales, size, base, offs):
    idx = unstriped(offs)
    keysu = unpack_weight(keys_words, keys_scales, "e4m3")
    valsu = unpack_weight(vals_words, vals_scales, "e4m3")
    queryq = mxq(f64(query), 0, "e4m3")
    keysidxg = keysu[:, idx]
    a = queryq.T @ keysidxg
    p = softplus(a - f64(th))
    z = np.sum(p, axis=1, keepdims=True) + f64(reserve)
    goutq = mxq(f64(gout), 0, "e4m3")
    valsidxg = valsu[:, idx]
    c0 = goutq.T @ valsidxg
    dz = np.sum(c0 * p * f64(size) / np.square(z) * (-1.0), axis=1, keepdims=True)
    dp = c0 / z * f64(size) + dz
    da = dp * sigmoid(a - f64(th))
    hda = da * 512.0 * 2.0 * 512.0
    hdp = hda * sigmoid(a - f64(th))
    hdz = np.sum(hdp, axis=1, keepdims=True)
    hz = np.sum(hdp * f64(size) * c0 / np.square(z) * (-1.0), axis=1, keepdims=True) + np.sum(hdz * (-1.0) * c0 * p * f64(size) / np.square(np.square(z)) * (-1.0), axis=1, keepdims=True) * z * 2.0
    hp = hdz * (-1.0) / np.square(z) * c0 * f64(size) + hz
    ha = hda * dp * sigmoid(a - f64(th)) * (1.0 - sigmoid(a - f64(th))) + hp * sigmoid(a - f64(th))
    y = ha + f64(base)
    return y

from contextlib import ExitStack

import concourse.mybir as mybir
from concourse.masks import make_identity

D, E, T, I, Q = 512, 512, 2048, 512, 128
FLOPS = 2 * Q * I * (D + E)

F32 = mybir.dt.float32
BF16 = mybir.dt.bfloat16
I32 = mybir.dt.int32
U32 = mybir.dt.uint32
U16 = mybir.dt.uint16
U8 = mybir.dt.uint8
FP8X4 = mybir.dt.float8_e4m3fn_x4
ALU = mybir.AluOpType
ACT = mybir.ActivationFunctionType

P = 128
PACK = 4
HALF = I // 2
PENALTY = 2.0 * 512.0 * 512.0
VALS_PLANE = 4


def tile_attend_gpsoftthreshold_kernel(
    tc, query, keys_words, keys_scales, th, reserve, gout, vals_words, vals_scales, size, base, offs, out
):
    nc = tc.nc
    halves = [slice(h * HALF, (h + 1) * HALF) for h in range(2)]

    with ExitStack() as ctx:
        sb = ctx.enter_context(tc.tile_pool(name="sb", bufs=1))
        ps = ctx.enter_context(tc.psum_pool(name="ps", bufs=1))

        def tile(name, width, dtype=F32, tag=None):
            return sb.tile([P, width], dtype, name=name, tag=tag or name, align_bytes=64)

        offsets = sb.tile([P, I // 16], U16, name="offsets")
        key_pool = tile("key_pool", T, U32)
        val_pool = tile("val_pool", T, U32)
        key_scale_pool = tile("key_scale_pool", T, U8)
        val_scale_pool = tile("val_scale_pool", T, U8)
        query_rows = tile("query_rows", PACK * Q)
        gout_rows = tile("gout_rows", PACK * Q)
        size_cols = tile("size_cols", PACK)
        th_col = tile("th_col", 1)
        reserve_col = tile("reserve_col", 1)
        base_sb = tile("base_sb", I)
        zero_col = tile("zero_col", 1)
        ident = tile("ident", P)

        nc.vector.memset(key_scale_pool[:].bitcast(I32), 0)
        nc.vector.memset(zero_col[:], 0.0)
        nc.vector.memset(val_scale_pool[:].bitcast(I32), 0)
        nc.vector.memset(ident[:], 0.0)
        make_identity(nc, ident[:], nomemset=True)

        warm = tile("warm", 1)
        nc.scalar.activation(warm[:], zero_col[:], ACT.Sigmoid)

        def load_rows(dst, src):
            nc.sync.dma_start(dst[:], src.rearrange("(p j) q -> p (j q)", j=PACK))

        def load_words(dst, src):
            nc.sync.dma_start(dst[:].bitcast(I32), src[0].rearrange("p n t -> p (n t)").bitcast(I32))

        def load_scales(dst, src, first):
            rows = src[0].bitcast(I32)
            words = dst[:].bitcast(I32)
            for quad in range(4):
                nc.sync.dma_start(words[32 * quad + first : 32 * quad + first + 4, :], rows[4 * quad : 4 * quad + 4, :])

        nc.sync.dma_start(offsets[:], offs)
        load_rows(query_rows, query)
        load_rows(gout_rows, gout)
        nc.sync.dma_start(size_cols[:], size.rearrange("o (p j) -> (o p) j", j=PACK))
        load_scales(key_scale_pool, keys_scales, 0)
        load_words(key_pool, keys_words)
        nc.sync.dma_start(th_col[:], th)
        load_scales(val_scale_pool, vals_scales, VALS_PLANE)
        load_words(val_pool, vals_words)
        nc.sync.dma_start(reserve_col[:], reserve)
        nc.sync.dma_start(base_sb[:], base)

        grouped = tile("grouped", 2 * Q * PACK, BF16)
        for n, rows in enumerate((query_rows, gout_rows)):
            nc.scalar.copy(
                grouped[:, n * Q * PACK : (n + 1) * Q * PACK].rearrange("p (c i t) -> p c t i", i=4, t=PACK),
                rows[:].rearrange("p (t c i) -> p c t i", i=4, t=PACK),
            )
        row_codes = tile("row_codes", 2 * Q, U32)
        row_scales = tile("row_scales", 2 * Q, U8)

        def gather_scales(name, pool):
            picked = tile(name, I, U8)
            nc.vector.tensor_copy(picked[:], pool[:].indirect(offsets[:]))
            return picked

        def product(name, pool, scales, first, codes, code_scales):
            picked = tile(name + "_words", I, U32)
            banks = []
            for h, cols in enumerate(halves):
                nc.vector.tensor_copy(picked[:, cols], pool[:].indirect(offsets[:, h * HALF // 16 : (h + 1) * HALF // 16]))
                bank = ps.tile([P, HALF], F32, name=name + "_bank%d" % h)
                nc.tensor.matmul_mx(
                    out=bank[:],
                    lhsT=codes.bitcast(FP8X4),
                    lhsT_scale=code_scales,
                    rhs=picked[:, cols].bitcast(FP8X4),
                    rhs_scale=scales[first:P, cols],
                    start=True,
                    stop=True,
                )
                banks.append(bank)
            return banks

        key_scales = gather_scales("key_scales", key_scale_pool)
        nc.vector.quantize_mx(out=row_codes[:].bitcast(FP8X4), scales=row_scales[:], in_=grouped[:])

        size_bank = ps.tile([P, PACK, P], F32, name="size_bank")
        for j in range(PACK):
            nc.tensor.transpose(size_bank[:, j, :], size_cols[:, j : j + 1].to_broadcast([P, P]), ident[:])
        size_sb = tile("size_sb", I)
        nc.scalar.copy(size_sb[:].rearrange("m (p j) -> m p j", j=PACK), size_bank[:].rearrange("m j p -> m p j"))

        neg_th = tile("neg_th", 1)
        nc.scalar.activation(neg_th[:], th_col[:], ACT.Identity, scale=-1.0)

        score_banks = product("score", key_pool, key_scales, 0, row_codes[:, 0:Q], row_scales[:, 0:Q])
        sig = tile("sig", I)
        off_mid = tile("off_mid", I)
        for cols, bank in zip(halves, score_banks):
            nc.scalar.activation(sig[:, cols], bank[:], ACT.Sigmoid, bias=neg_th[:])
            nc.scalar.activation(off_mid[:, cols], sig[:, cols], ACT.Abs, bias=-0.5)
        log_top = tile("log_top", I)
        sum_log = tile("sum_log", 1)
        nc.scalar.activation(log_top[:], off_mid[:], ACT.Ln, bias=0.5, accum_out=sum_log[:])

        val_scales = gather_scales("val_scales", val_scale_pool)
        grad_banks = product("grad", val_pool, val_scales, VALS_PLANE, row_codes[:, Q : 2 * Q], row_scales[:, Q : 2 * Q])

        relu = tile("relu", I, tag="val_pool")
        sum_relu = tile("sum_relu", 2)
        for h, (cols, bank) in enumerate(zip(halves, score_banks)):
            nc.vector.scalar_tensor_tensor(
                relu[:, cols], bank[:], th_col[:], zero_col[:].to_broadcast([P, HALF]), ALU.subtract, ALU.max,
                accum_out=sum_relu[:, h : h + 1],
            )
        c = tile("c", I)
        for cols, bank in zip(halves, grad_banks):
            nc.vector.tensor_tensor(c[:, cols], bank[:], size_sb[:, cols], ALU.mult)

        z_relu = tile("z_relu", 1)
        nc.vector.tensor_scalar(z_relu[:], sum_relu[:, 0:1], sum_relu[:, 1:2], reserve_col[:], ALU.add, ALU.add)
        z = tile("z", 1)
        nc.scalar.activation(z[:], sum_log[:], ACT.Identity, scale=-1.0, bias=z_relu[:])
        rest = tile("rest", I)
        nc.scalar.activation(rest[:], sig[:], ACT.Identity, scale=-1.0, bias=1.0)

        cp = tile("cp", I)
        cl = tile("cl", I)
        cp_sums = tile("cp_sums", 2)
        nc.vector.scalar_tensor_tensor(cp[:], c[:], 1.0, relu[:], ALU.mult, ALU.mult, accum_out=cp_sums[:, 0:1])
        nc.vector.scalar_tensor_tensor(cl[:], c[:], -1.0, log_top[:], ALU.mult, ALU.mult, accum_out=cp_sums[:, 1:2])
        r = tile("r", 1)
        nc.vector.reciprocal(r[:], z[:])
        mean_parts = tile("mean_parts", 2)
        mean = tile("mean", 1)
        nc.vector.tensor_scalar(mean_parts[:], cp_sums[:], r[:], None, ALU.mult, ALU.add, accum_out=mean[:])

        r2 = tile("r2", 1)
        neg_k2 = tile("neg_k2", 1)
        neg_k3 = tile("neg_k3", 1)
        nc.scalar.activation(r2[:], r[:], ACT.Square)
        nc.scalar.activation(neg_k2[:], r2[:], ACT.Identity, scale=-PENALTY)
        nc.scalar.activation(neg_k3[:], neg_k2[:], ACT.Identity, scale=r[:])

        w = tile("w", I)
        w2 = tile("w2", I)
        neg_wo = tile("neg_wo", I)
        ws_sums = tile("ws_sums", 4)
        w2_sums = tile("w2_sums", 2)
        for h, cols in enumerate(halves):
            nc.vector.scalar_tensor_tensor(
                w[:, cols], c[:, cols], mean[:], sig[:, cols], ALU.subtract, ALU.mult, accum_out=ws_sums[:, h : h + 1]
            )
            nc.scalar.activation(w2[:, cols], w[:, cols], ACT.Square, accum_out=w2_sums[:, h : h + 1])
        for h, cols in enumerate(halves):
            nc.vector.scalar_tensor_tensor(
                neg_wo[:, cols], w[:, cols], -1.0, rest[:, cols], ALU.mult, ALU.mult, accum_out=ws_sums[:, 2 + h : 3 + h]
            )
        gamma_parts = tile("gamma_parts", 2)
        neg_gamma = tile("neg_gamma", 1)
        nc.scalar.activation(gamma_parts[:], w2_sums[:], ACT.Identity, scale=neg_k3[:], accum_out=neg_gamma[:])
        beta_parts = tile("beta_parts", 4)
        beta = tile("beta", 1)
        nc.vector.tensor_scalar(beta_parts[:], ws_sums[:], r[:], None, ALU.mult, ALU.add, accum_out=beta[:])

        shifted = tile("shifted", I)
        nc.vector.scalar_tensor_tensor(shifted[:], sig[:], neg_gamma[:], base_sb[:], ALU.mult, ALU.add)
        quad = tile("quad", I)
        result = tile("result", I)
        for cols in halves:
            nc.vector.scalar_tensor_tensor(quad[:, cols], neg_wo[:, cols], beta[:], w[:, cols], ALU.add, ALU.mult)
        for cols, queue in zip(halves, (nc.sync, nc.scalar)):
            nc.vector.scalar_tensor_tensor(result[:, cols], quad[:, cols], neg_k2[:], shifted[:, cols], ALU.mult, ALU.add)
            queue.dma_start(out[:, cols], result[:, cols])
